import numpy as np
import ml_dtypes


def mxq(x, axis, fmt="e4m3"):
    dtype, down = {"e4m3": (ml_dtypes.float8_e4m3fn, 7), "e5m2": (ml_dtypes.float8_e5m2, 14)}[fmt]
    v = np.moveaxis(np.asarray(x, np.float32).astype(ml_dtypes.bfloat16).astype(np.float64), axis, -1)
    blocks = v.reshape(v.shape[:-1] + (-1, 32))
    amax = np.abs(blocks).max(-1, keepdims=True)
    byte = np.maximum(np.where(amax > 0, np.frexp(amax)[1] - 1 + 127, 0) - down, 1)
    scale = np.exp2(byte - 127.0)
    codes = (blocks / scale).astype(np.float32).astype(dtype).astype(np.float64)
    return np.moveaxis((codes * scale).reshape(v.shape), -1, axis)


WIDE = False


def mx_kscale(k):
    if not WIDE:
        return np.ones(k)
    levels = np.array([10, -10, 5, -5, 0])
    if k % 512:
        return np.exp2(np.random.permutation(np.resize(levels, k // 32))).repeat(32)
    a = np.empty((k // 512, 16))
    for p in range(k // 512):
        a[p, :8] = np.random.permutation(np.resize(levels, 8))
        for g in range(8):
            far = levels[np.abs(levels - a[p, g]) >= 10]
            a[p, g + 8] = far[np.random.randint(len(far))]
    return np.exp2(a.ravel()).repeat(32)


def f64(x):
    return np.asarray(x).astype(np.float64)


def striped(idx):
    return np.tile(idx.reshape(-1, 16).T, (8, 1)).astype(np.uint16)


def unstriped(offs):
    return offs[:16].T.reshape(-1).astype(np.int64)


def pack_weight(w):
    k, n = w.shape
    w = f64(np.asarray(w, np.float32).astype(ml_dtypes.bfloat16)).reshape(k // 32, 32, n)
    amax = np.abs(w).max(1)
    byte = np.clip(np.where(amax > 0, np.frexp(amax)[1] - 1 + 127 - 7, 1), 1, 254)
    scaled = (w * np.exp2(127.0 - byte)[:, None, :]).reshape(k, n).astype(np.float32)
    words = np.ascontiguousarray(scaled.reshape(k // 512, 128, 4, n).transpose(0, 1, 3, 2)).astype(ml_dtypes.float8_e4m3fn).view(np.uint8)
    return words, np.ascontiguousarray(byte.astype(np.uint8).reshape(k // 512, 16, n))


def unpack_weight(words, scales):
    g, p, n, _ = words.shape
    vals = np.ascontiguousarray(words).view(ml_dtypes.float8_e4m3fn).astype(np.float64) * np.repeat(np.exp2(scales.astype(np.float64) - 127.0), 8, axis=1)[..., None]
    return vals.transpose(0, 1, 3, 2).reshape(g * 512, n)


K, T, S, D, H, Z, W = 512, 2048, 512, 2, 512, 512, 2048
P = 2 ** 7


def setup_inputs():
    n = np.random.standard_normal
    s = mx_kscale(K)[:, None]
    u = mx_kscale(H)
    packed_xT = pack_weight(n((K, T)) * s)
    packed_eT = pack_weight(n((K, W)) * s)
    return {
        "x_words": packed_xT[0],
        "x_scales": packed_xT[1],
        "w1": (n((K, H)) / np.sqrt(K) / s).astype(np.float32),
        "e_words": packed_eT[0],
        "e_scales": packed_eT[1],
        "w2": (n((K, H)) / np.sqrt(K) / s).astype(np.float32),
        "unit": (np.random.uniform(0.6, 1.4, (H, 1)) * u[:, None]).astype(np.float32),
        "unit2": (np.random.uniform(0.6, 1.4, (H, 1)) / np.sqrt(H) / u[:, None]).astype(np.float32),
        "fert": (np.tile(np.random.uniform(0.4, 1.6, W), (P, 1))).astype(np.float32),
        "offs": striped(np.random.permutation(T)[:S]),
        "tgt": striped(np.random.permutation(W)[:Z]),
        "mor": striped(np.random.permutation(Z)),
        "dia": striped(np.random.permutation(Z)),
    }


def reference(x_words, x_scales, w1, e_words, e_scales, w2, unit, unit2, fert, offs, tgt, mor, dia):
    xq = unpack_weight(x_words, x_scales)[:, unstriped(offs)]
    y = mxq(f64(w1), 0, "e4m3").T @ xq
    word = y.reshape(len(y), -1, D).max(axis=2) + 0.5 * (y.reshape(len(y), -1, D).min(axis=2))
    hid = f64(unit) * word
    e_tgt = unpack_weight(e_words, e_scales)[:, unstriped(tgt)]
    ye = mxq(f64(w2), 0, "e4m3").T @ e_tgt
    em_ = ye[:, unstriped(mor)]
    tw = np.maximum(ye, 0.7 * em_)
    hid2 = f64(unit2) * tw
    sc = mxq(hid, 0, "e4m3").T @ mxq(hid2, 0, "e4m3")
    top = sc.max(axis=1, keepdims=True)
    ew = np.exp(sc - top)
    tot = ew.sum(axis=1, keepdims=True)
    pr = 50.0 * (ew / tot)
    return pr * (f64(fert)[:1][:, unstriped(tgt)]) - (0.5 * pr[:, unstriped(dia)])

@@ -1,0 +1,231 @@
+from contextlib import ExitStack
+
+import concourse.mybir as mybir
+
+F32 = mybir.dt.float32
+BF16 = mybir.dt.bfloat16
+I32 = mybir.dt.int32
+U32 = mybir.dt.uint32
+U16 = mybir.dt.uint16
+U8 = mybir.dt.uint8
+FP8X4 = mybir.dt.float8_e4m3fn_x4
+ALU = mybir.AluOpType
+ACT = mybir.ActivationFunctionType
+
+P = 128
+PACK = 4
+TABLE = 2048
+PICKED = 512
+HALF = 256
+LIST_COLS = PICKED // 16
+HALF_COLS = HALF // 16
+
+FLOPS = 2 * 512 * 512 * 512 * 2 + 2 * 256 * 512 * 512
+
+
+def tile_picked_ywordal_fert_p_kernel(
+    tc, x_words, x_scales, w1, e_words, e_scales, w2, unit, unit2, fert, offs, tgt, mor, dia, out
+):
+    nc = tc.nc
+    with ExitStack() as ctx:
+        sb = ctx.enter_context(tc.tile_pool(name="sb", bufs=1))
+        ps = ctx.enter_context(tc.psum_pool(name="ps", bufs=1))
+
+        def load_list(src, name):
+            t = sb.tile([P, LIST_COLS], U16, name=name)
+            nc.sync.dma_start(t[:], src)
+            return t
+
+        def load_words(src, name):
+            t = sb.tile([P, TABLE], I32, name=name, tag=name, align_bytes=64)
+            nc.sync.dma_start(t[:], src[0].rearrange("p n r -> p (n r)").bitcast(I32))
+            return t
+
+        def load_scales(src, name, clear, queue):
+            t = sb.tile([P, TABLE], U8, name=name, tag=name, align_bytes=64)
+            clear.memset(t[:].bitcast(I32), 0)
+            for q in range(4):
+                queue.dma_start(t[32 * q : 32 * q + 4, :].bitcast(I32), src[0, 4 * q : 4 * q + 4, :].bitcast(I32))
+            return t
+
+        def load_weight(src, name):
+            t = sb.tile([P, PACK, PICKED], F32, name=name)
+            nc.sync.dma_start(t[:], src.rearrange("(p j) c -> p j c", j=PACK))
+            return t
+
+        def load_factor(src, name):
+            t = sb.tile([P, PACK], F32, name=name)
+            nc.sync.dma_start(t[:], src.rearrange("(p t) o -> p (t o)", t=PACK))
+            return t
+
+        e_scale_tab = load_scales(e_scales, "e_scale_tab", nc.gpsimd, nc.scalar)
+        tgt_t = load_list(tgt, "tgt_t")
+        unit2_t = load_factor(unit2, "unit2_t")
+        mor_t = load_list(mor, "mor_t")
+        w2_raw = load_weight(w2, "w2_raw")
+        e_word_tab = load_words(e_words, "e_word_tab")
+        x_scale_tab = load_scales(x_scales, "x_scale_tab", nc.gpsimd, nc.gpsimd)
+        w1_raw = load_weight(w1, "w1_raw")
+        x_word_tab = load_words(x_words, "x_word_tab")
+        offs_t = load_list(offs, "offs_t")
+        unit_t = load_factor(unit, "unit_t")
+        dia_t = load_list(dia, "dia_t")
+        fert_tab = sb.tile([P, TABLE], F32, name="fert_tab")
+        nc.sync.dma_start(fert_tab[:], fert)
+
+        def round_weight(raw, name, tag):
+            grouped = sb.tile([P, PACK * PICKED], BF16, name=name, tag=tag, align_bytes=64)
+            nc.vector.tensor_copy(
+                grouped[:].rearrange("p (t m j) -> p m j t", t=PACK, j=PACK), raw[:].rearrange("p j (m t) -> p m j t", t=PACK)
+            )
+            return grouped
+
+        def quantise_weight(grouped, name):
+            codes = sb.tile([P, PICKED], U32, name=name + "_codes", align_bytes=64)
+            scales = sb.tile([P, PICKED], U8, name=name + "_scales", align_bytes=64)
+            nc.vector.quantize_mx(out=codes[:].bitcast(FP8X4), scales=scales[:], in_=grouped[:])
+            return codes, scales
+
+        e_bytes = sb.tile([P, PICKED], U8, name="e_bytes", align_bytes=64)
+        nc.vector.tensor_copy(e_bytes[:], e_scale_tab[:].indirect(tgt_t[:]))
+        two_if_pos = sb.tile([P, PACK], F32, name="two_if_pos")
+        nc.vector.tensor_scalar(two_if_pos[:], unit2_t[:], 0.0, 2.0, ALU.is_ge, ALU.mult)
+        abs_unit2 = sb.tile([P, PACK], F32, name="abs_unit2")
+        nc.vector.scalar_tensor_tensor(abs_unit2[:], two_if_pos[:], -1.0, unit2_t[:], ALU.add, ALU.mult)
+        w2_codes, w2_scales = quantise_weight(round_weight(w2_raw, "w2_grouped", "w2_grouped"), "w2")
+        e_codes = sb.tile([P, PICKED], U32, name="e_codes", align_bytes=64)
+        nc.vector.tensor_copy(e_codes[:], e_word_tab[:].bitcast(U32).indirect(tgt_t[:]))
+        x_bytes = sb.tile([P, PICKED], U8, name="x_bytes", tag="e_word_tab", align_bytes=64)
+        nc.vector.tensor_copy(x_bytes[:], x_scale_tab[:].indirect(offs_t[:]))
+
+        ye = sb.tile([P, PACK, PICKED], F32, name="ye")
+        for t in range(PACK):
+            bank = ps.tile([P, PICKED], F32, name="ye_bank%d" % t, tag="bank%d" % t)
+            cols = slice(P * t, P * (t + 1))
+            nc.tensor.matmul_mx(
+                out=bank[:], lhsT=w2_codes[:, cols].bitcast(FP8X4), lhsT_scale=w2_scales[:, cols],
+                rhs=e_codes[:].bitcast(FP8X4), rhs_scale=e_bytes[:], start=True, stop=True,
+            )
+            if t == PACK - 1:
+                nc.vector.tensor_scalar(ye[:, t, :], bank[:], abs_unit2[:, t : t + 1], None, ALU.mult)
+            else:
+                nc.scalar.activation(ye[:, t, :], bank[:], ACT.Copy, scale=abs_unit2[:, t : t + 1])
+
+        related = []
+        for u in range(2):
+            rel = sb.tile([P, PACK, HALF], F32, name="related%d" % u)
+            for t in range(PACK):
+                nc.scalar.activation(
+                    rel[:, t, :], ye[:, t, :].indirect(mor_t[:, HALF_COLS * u : HALF_COLS * (u + 1)]), ACT.Copy, scale=0.7
+                )
+            related.append(rel)
+
+        w1_codes, w1_scales = quantise_weight(round_weight(w1_raw, "w1_grouped", "x_scale_tab"), "w1")
+        x_codes = sb.tile([P, PICKED], U32, name="x_codes", tag="x_scale_tab", align_bytes=64)
+        y_banks = []
+        for h in range(2):
+            picks = slice(HALF * h, HALF * (h + 1))
+            nc.vector.tensor_copy(
+                x_codes[:, picks], x_word_tab[:].bitcast(U32).indirect(offs_t[:, HALF_COLS * h : HALF_COLS * (h + 1)])
+            )
+            pair = []
+            for b in range(2):
+                bank = ps.tile([P, 2, HALF], F32, name="y_bank%d%d" % (h, b), tag="bank%d" % (4 + 2 * h + b))
+                for s in range(2):
+                    cols = slice(P * (2 * b + s), P * (2 * b + s + 1))
+                    nc.tensor.matmul_mx(
+                        out=bank[:, s, :], lhsT=w1_codes[:, cols].bitcast(FP8X4), lhsT_scale=w1_scales[:, cols],
+                        rhs=x_codes[:, picks].bitcast(FP8X4), rhs_scale=x_bytes[:, picks],
+                        start=True, stop=True,
+                    )
+                pair.append(bank)
+            y_banks.append(pair)
+
+        signed_unit = sb.tile([P, PACK], F32, name="signed_unit")
+        nc.vector.scalar_tensor_tensor(signed_unit[:], two_if_pos[:], -1.0, unit_t[:], ALU.add, ALU.mult)
+        for_max = sb.tile([P, PACK], F32, name="for_max")
+        nc.vector.scalar_tensor_tensor(for_max[:], signed_unit[:], 0.5, signed_unit[:], ALU.mult, ALU.max)
+        for_min = sb.tile([P, PACK], F32, name="for_min")
+        nc.vector.scalar_tensor_tensor(for_min[:], signed_unit[:], 0.5, signed_unit[:], ALU.mult, ALU.min)
+
+        hid2 = sb.tile([P, PACK * PICKED], BF16, name="hid2", tag="x_word_tab", align_bytes=64)
+        hid2_codes = sb.tile([P, PICKED], U32, name="hid2_codes", align_bytes=64)
+        hid2_scales = sb.tile([P, PICKED], U8, name="hid2_scales", align_bytes=64)
+        for u in range(2):
+            cols = slice(HALF * u, HALF * (u + 1))
+            part = hid2[:, PACK * HALF * u : PACK * HALF * (u + 1)]
+            nc.vector.tensor_tensor(
+                part.rearrange("p (c i t) -> p c t i", i=4, t=PACK),
+                ye[:, :, cols].rearrange("p t (c i) -> p c t i", i=4),
+                related[u][:].rearrange("p t (c i) -> p c t i", i=4),
+                ALU.max,
+            )
+            nc.vector.quantize_mx(out=hid2_codes[:, cols].bitcast(FP8X4), scales=hid2_scales[:, cols], in_=part)
+
+        def pairs_of(h, t):
+            return y_banks[h][t // 2][:].rearrange("p s (v d) -> p s d v", d=2)[:, t % 2]
+
+        odd = []
+        for h in range(2):
+            odd_max = sb.tile([P, PACK, P], F32, name="odd_max%d" % h, tag="odd_max%d" % h)
+            odd_min = sb.tile([P, PACK, P], F32, name="odd_min%d" % h)
+            for t in range(PACK):
+                nc.scalar.activation(odd_max[:, t, :], pairs_of(h, t)[:, 1, :], ACT.Copy, scale=for_max[:, t : t + 1])
+                nc.scalar.activation(odd_min[:, t, :], pairs_of(h, t)[:, 1, :], ACT.Copy, scale=for_min[:, t : t + 1])
+            odd.append((odd_max, odd_min))
+
+        def scores(h):
+            larger = sb.tile([P, PACK, P], F32, name="larger%d" % h)
+            smaller = sb.tile([P, PACK, P], F32, name="smaller%d" % h)
+            for t in range(PACK):
+                even = pairs_of(h, t)[:, 0, :]
+                nc.vector.scalar_tensor_tensor(larger[:, t, :], even, for_max[:, t : t + 1], odd[h][0][:, t, :], ALU.mult, ALU.max)
+                nc.vector.scalar_tensor_tensor(smaller[:, t, :], even, for_min[:, t : t + 1], odd[h][1][:, t, :], ALU.mult, ALU.min)
+            hid = sb.tile([P, PACK * P], BF16, name="hid%d" % h, align_bytes=64)
+            nc.vector.tensor_tensor(
+                hid[:].rearrange("p (c i t) -> p c t i", i=4, t=PACK),
+                larger[:].rearrange("p t (c i) -> p c t i", i=4),
+                smaller[:].rearrange("p t (c i) -> p c t i", i=4),
+                ALU.add,
+            )
+            hid_codes = sb.tile([P, P], U32, name="hid_codes%d" % h, align_bytes=64)
+            hid_scales = sb.tile([P, P], U8, name="hid_scales%d" % h, align_bytes=64)
+            nc.vector.quantize_mx(out=hid_codes[:].bitcast(FP8X4), scales=hid_scales[:], in_=hid[:])
+            sc = ps.tile([P, PICKED], F32, name="sc%d" % h, tag="bank%d" % h)
+            nc.tensor.matmul_mx(
+                out=sc[:], lhsT=hid_codes[:].bitcast(FP8X4), lhsT_scale=hid_scales[:],
+                rhs=hid2_codes[:].bitcast(FP8X4), rhs_scale=hid2_scales[:], start=True, stop=True,
+            )
+            return sc
+
+        def exponentials(h, sc):
+            neg_top = sb.tile([P, 1], F32, name="neg_top%d" % h)
+            nc.vector.tensor_reduce(neg_top[:], sc[:], mybir.AxisListType.X, ALU.max, negate=True)
+            ew = sb.tile([P, PICKED], F32, name="ew%d" % h)
+            tot = sb.tile([P, 1], F32, name="tot%d" % h)
+            nc.scalar.activation(ew[:], sc[:], ACT.Exp, bias=neg_top[:], accum_out=tot[:])
+            other = sb.tile([P, PICKED], F32, name="other%d" % h)
+            for u in range(2):
+                nc.scalar.activation(
+                    other[:, HALF * u : HALF * (u + 1)],
+                    ew[:].indirect(dia_t[:, HALF_COLS * u : HALF_COLS * (u + 1)]), ACT.Copy, scale=-25.0,
+                )
+            return ew, tot, other
+
+        def finish(h, ew, tot, other):
+            inv_tot = sb.tile([P, 1], F32, name="inv_tot%d" % h)
+            nc.vector.reciprocal(inv_tot[:], tot[:])
+            own = sb.tile([P, PICKED], F32, name="own%d" % h)
+            nc.vector.scalar_tensor_tensor(own[:], ew[:], inv_tot[:], fert50[:], ALU.mult, ALU.mult)
+            res = sb.tile([P, PICKED], F32, name="res%d" % h)
+            nc.vector.scalar_tensor_tensor(res[:], other[:], inv_tot[:], own[:], ALU.mult, ALU.add)
+            nc.sync.dma_start(out[P * h : P * (h + 1), :], res[:])
+
+        sc0 = scores(0)
+        fert50 = sb.tile([P, PICKED], F32, name="fert50", tag="odd_max0")
+        nc.scalar.activation(fert50[:], fert_tab[:].indirect(tgt_t[:]), ACT.Copy, scale=50.0)
+        soft0 = exponentials(0, sc0)
+        sc1 = scores(1)
+        soft1 = exponentials(1, sc1)
+        finish(0, *soft0)
+        finish(1, *soft1)

@@ -36,8 +36,8 @@ def tile_picked_ywordal_fert_p_kernel(
             nc.sync.dma_start(t[:], src)
             return t
 
-        def load_words(src, name):
-            t = sb.tile([P, TABLE], I32, name=name, tag=name, align_bytes=64)
+        def load_words(src, name, tag):
+            t = sb.tile([P, TABLE], I32, name=name, tag=tag, align_bytes=64)
             nc.sync.dma_start(t[:], src[0].rearrange("p n r -> p (n r)").bitcast(I32))
             return t
 
@@ -48,36 +48,41 @@ def tile_picked_ywordal_fert_p_kernel(
                 queue.dma_start(t[32 * q : 32 * q + 4, :].bitcast(I32), src[0, 4 * q : 4 * q + 4, :].bitcast(I32))
             return t
 
-        def load_weight(src, name):
-            t = sb.tile([P, PACK, PICKED], F32, name=name)
+        def load_weight(src, name, tag):
+            t = sb.tile([P, PACK, PICKED], F32, name=name, tag=tag, align_bytes=64)
             nc.sync.dma_start(t[:], src.rearrange("(p j) c -> p j c", j=PACK))
             return t
 
         def load_factor(src, name):
-            t = sb.tile([P, PACK], F32, name=name)
+            t = sb.tile([P, PACK], F32, name=name, tag=name, align_bytes=64)
             nc.sync.dma_start(t[:], src.rearrange("(p t) o -> p (t o)", t=PACK))
             return t
 
         e_scale_tab = load_scales(e_scales, "e_scale_tab", nc.gpsimd, nc.scalar)
         tgt_t = load_list(tgt, "tgt_t")
         unit2_t = load_factor(unit2, "unit2_t")
+        w2_raw = load_weight(w2, "w2_raw", "w2_raw")
+        e_word_tab = load_words(e_words, "e_word_tab", "e_word_tab")
+        x_scale_tab = load_scales(x_scales, "x_scale_tab", nc.gpsimd, nc.scalar)
         mor_t = load_list(mor, "mor_t")
-        w2_raw = load_weight(w2, "w2_raw")
-        e_word_tab = load_words(e_words, "e_word_tab")
-        x_scale_tab = load_scales(x_scales, "x_scale_tab", nc.gpsimd, nc.gpsimd)
-        w1_raw = load_weight(w1, "w1_raw")
-        x_word_tab = load_words(x_words, "x_word_tab")
         offs_t = load_list(offs, "offs_t")
+        w1_raw = load_weight(w1, "w1_raw", "w1_raw")
+        x_word_tab = load_words(x_words, "x_word_tab", "x_word_tab")
         unit_t = load_factor(unit, "unit_t")
         dia_t = load_list(dia, "dia_t")
-        fert_tab = sb.tile([P, TABLE], F32, name="fert_tab")
-        nc.sync.dma_start(fert_tab[:], fert)
 
-        def round_weight(raw, name, tag):
+        two_if_pos = sb.tile([P, PACK], F32, name="two_if_pos")
+        nc.vector.tensor_scalar(two_if_pos[:], unit2_t[:], 0.0, 2.0, ALU.is_ge, ALU.mult)
+        abs_unit2 = sb.tile([P, PACK], F32, name="abs_unit2")
+        nc.vector.scalar_tensor_tensor(abs_unit2[:], two_if_pos[:], -1.0, unit2_t[:], ALU.add, ALU.mult)
+
+        def round_weight(raw, name, tag, split):
             grouped = sb.tile([P, PACK * PICKED], BF16, name=name, tag=tag, align_bytes=64)
-            nc.vector.tensor_copy(
-                grouped[:].rearrange("p (t m j) -> p m j t", t=PACK, j=PACK), raw[:].rearrange("p j (m t) -> p m j t", t=PACK)
-            )
+            dst = grouped[:].rearrange("p (t m j) -> p m j t", t=PACK, j=PACK)
+            src = raw[:].rearrange("p j (m t) -> p m j t", t=PACK)
+            nc.vector.tensor_copy(dst[:, :split], src[:, :split])
+            if split < P:
+                nc.scalar.copy(dst[:, split:], src[:, split:])
             return grouped
 
         def quantise_weight(grouped, name):
@@ -88,11 +93,9 @@ def tile_picked_ywordal_fert_p_kernel(
 
         e_bytes = sb.tile([P, PICKED], U8, name="e_bytes", align_bytes=64)
         nc.vector.tensor_copy(e_bytes[:], e_scale_tab[:].indirect(tgt_t[:]))
-        two_if_pos = sb.tile([P, PACK], F32, name="two_if_pos")
-        nc.vector.tensor_scalar(two_if_pos[:], unit2_t[:], 0.0, 2.0, ALU.is_ge, ALU.mult)
-        abs_unit2 = sb.tile([P, PACK], F32, name="abs_unit2")
-        nc.vector.scalar_tensor_tensor(abs_unit2[:], two_if_pos[:], -1.0, unit2_t[:], ALU.add, ALU.mult)
-        w2_codes, w2_scales = quantise_weight(round_weight(w2_raw, "w2_grouped", "w2_grouped"), "w2")
+        w2_codes, w2_scales = quantise_weight(round_weight(w2_raw, "w2_grouped", "w2_grouped", P), "w2")
+        fert_tab = sb.tile([P, TABLE], F32, name="fert_tab", tag="w2_raw", align_bytes=64)
+        nc.sync.dma_start(fert_tab[:], fert)
         e_codes = sb.tile([P, PICKED], U32, name="e_codes", align_bytes=64)
         nc.vector.tensor_copy(e_codes[:], e_word_tab[:].bitcast(U32).indirect(tgt_t[:]))
         x_bytes = sb.tile([P, PICKED], U8, name="x_bytes", tag="e_word_tab", align_bytes=64)
@@ -120,7 +123,7 @@ def tile_picked_ywordal_fert_p_kernel(
                 )
             related.append(rel)
 
-        w1_codes, w1_scales = quantise_weight(round_weight(w1_raw, "w1_grouped", "x_scale_tab"), "w1")
+        w1_codes, w1_scales = quantise_weight(round_weight(w1_raw, "w1_grouped", "x_scale_tab", P), "w1")
         x_codes = sb.tile([P, PICKED], U32, name="x_codes", tag="x_scale_tab", align_bytes=64)
         y_banks = []
         for h in range(2):
@@ -141,7 +144,7 @@ def tile_picked_ywordal_fert_p_kernel(
                 pair.append(bank)
             y_banks.append(pair)
 
-        signed_unit = sb.tile([P, PACK], F32, name="signed_unit")
+        signed_unit = sb.tile([P, PACK], F32, name="signed_unit", tag="w1_raw", align_bytes=64)
         nc.vector.scalar_tensor_tensor(signed_unit[:], two_if_pos[:], -1.0, unit_t[:], ALU.add, ALU.mult)
         for_max = sb.tile([P, PACK], F32, name="for_max")
         nc.vector.scalar_tensor_tensor(for_max[:], signed_unit[:], 0.5, signed_unit[:], ALU.mult, ALU.max)

@@ -41,12 +41,14 @@ def tile_picked_ywordal_fert_p_kernel(
             nc.sync.dma_start(t[:], src[0].rearrange("p n r -> p (n r)").bitcast(I32))
             return t
 
-        def load_scales(src, name, clear, queue):
+        def cleared_scale_table(name):
             t = sb.tile([P, TABLE], U8, name=name, tag=name, align_bytes=64)
-            clear.memset(t[:].bitcast(I32), 0)
-            for q in range(4):
-                queue.dma_start(t[32 * q : 32 * q + 4, :].bitcast(I32), src[0, 4 * q : 4 * q + 4, :].bitcast(I32))
+            nc.vector.memset(t[:].bitcast(I32), 0)
             return t
+
+        def load_scales(t, src):
+            for r in range(4):
+                nc.sync.dma_start(t[r:P:32, :].bitcast(I32), src[0, r:16:4, :].bitcast(I32))
 
         def load_weight(src, name, tag):
             t = sb.tile([P, PACK, PICKED], F32, name=name, tag=tag, align_bytes=64)
@@ -58,150 +60,162 @@ def tile_picked_ywordal_fert_p_kernel(
             nc.sync.dma_start(t[:], src.rearrange("(p t) o -> p (t o)", t=PACK))
             return t
 
-        e_scale_tab = load_scales(e_scales, "e_scale_tab", nc.gpsimd, nc.scalar)
+        e_scale_tab = cleared_scale_table("e_scale_tab")
+        x_scale_tab = cleared_scale_table("x_scale_tab")
         tgt_t = load_list(tgt, "tgt_t")
         unit2_t = load_factor(unit2, "unit2_t")
-        w2_raw = load_weight(w2, "w2_raw", "w2_raw")
-        e_word_tab = load_words(e_words, "e_word_tab", "e_word_tab")
-        x_scale_tab = load_scales(x_scales, "x_scale_tab", nc.gpsimd, nc.scalar)
-        mor_t = load_list(mor, "mor_t")
-        offs_t = load_list(offs, "offs_t")
-        w1_raw = load_weight(w1, "w1_raw", "w1_raw")
-        x_word_tab = load_words(x_words, "x_word_tab", "x_word_tab")
         unit_t = load_factor(unit, "unit_t")
+        w2_raw = load_weight(w2, "w2_raw", "w2_raw")
+        load_scales(e_scale_tab, e_scales)
+        offs_t = load_list(offs, "offs_t")
+        mor_t = load_list(mor, "mor_t")
+        e_word_tab = load_words(e_words, "e_word_tab", "e_word_tab")
+        load_scales(x_scale_tab, x_scales)
+        w1_raw = load_weight(w1, "w1_raw", "w1_raw")
         dia_t = load_list(dia, "dia_t")
+        x_word_tab = load_words(x_words, "x_word_tab", "x_word_tab")
 
         two_if_pos = sb.tile([P, PACK], F32, name="two_if_pos")
         nc.vector.tensor_scalar(two_if_pos[:], unit2_t[:], 0.0, 2.0, ALU.is_ge, ALU.mult)
         abs_unit2 = sb.tile([P, PACK], F32, name="abs_unit2")
         nc.vector.scalar_tensor_tensor(abs_unit2[:], two_if_pos[:], -1.0, unit2_t[:], ALU.add, ALU.mult)
-
-        def round_weight(raw, name, tag, split):
-            grouped = sb.tile([P, PACK * PICKED], BF16, name=name, tag=tag, align_bytes=64)
-            dst = grouped[:].rearrange("p (t m j) -> p m j t", t=PACK, j=PACK)
-            src = raw[:].rearrange("p j (m t) -> p m j t", t=PACK)
-            nc.vector.tensor_copy(dst[:, :split], src[:, :split])
-            if split < P:
-                nc.scalar.copy(dst[:, split:], src[:, split:])
-            return grouped
-
-        def quantise_weight(grouped, name):
-            codes = sb.tile([P, PICKED], U32, name=name + "_codes", align_bytes=64)
-            scales = sb.tile([P, PICKED], U8, name=name + "_scales", align_bytes=64)
-            nc.vector.quantize_mx(out=codes[:].bitcast(FP8X4), scales=scales[:], in_=grouped[:])
-            return codes, scales
-
-        e_bytes = sb.tile([P, PICKED], U8, name="e_bytes", align_bytes=64)
-        nc.vector.tensor_copy(e_bytes[:], e_scale_tab[:].indirect(tgt_t[:]))
-        w2_codes, w2_scales = quantise_weight(round_weight(w2_raw, "w2_grouped", "w2_grouped", P), "w2")
-        fert_tab = sb.tile([P, TABLE], F32, name="fert_tab", tag="w2_raw", align_bytes=64)
-        nc.sync.dma_start(fert_tab[:], fert)
-        e_codes = sb.tile([P, PICKED], U32, name="e_codes", align_bytes=64)
-        nc.vector.tensor_copy(e_codes[:], e_word_tab[:].bitcast(U32).indirect(tgt_t[:]))
-        x_bytes = sb.tile([P, PICKED], U8, name="x_bytes", tag="e_word_tab", align_bytes=64)
-        nc.vector.tensor_copy(x_bytes[:], x_scale_tab[:].indirect(offs_t[:]))
-
-        ye = sb.tile([P, PACK, PICKED], F32, name="ye")
-        for t in range(PACK):
-            bank = ps.tile([P, PICKED], F32, name="ye_bank%d" % t, tag="bank%d" % t)
-            cols = slice(P * t, P * (t + 1))
-            nc.tensor.matmul_mx(
-                out=bank[:], lhsT=w2_codes[:, cols].bitcast(FP8X4), lhsT_scale=w2_scales[:, cols],
-                rhs=e_codes[:].bitcast(FP8X4), rhs_scale=e_bytes[:], start=True, stop=True,
-            )
-            if t == PACK - 1:
-                nc.vector.tensor_scalar(ye[:, t, :], bank[:], abs_unit2[:, t : t + 1], None, ALU.mult)
-            else:
-                nc.scalar.activation(ye[:, t, :], bank[:], ACT.Copy, scale=abs_unit2[:, t : t + 1])
-
-        related = []
-        for u in range(2):
-            rel = sb.tile([P, PACK, HALF], F32, name="related%d" % u)
-            for t in range(PACK):
-                nc.scalar.activation(
-                    rel[:, t, :], ye[:, t, :].indirect(mor_t[:, HALF_COLS * u : HALF_COLS * (u + 1)]), ACT.Copy, scale=0.7
-                )
-            related.append(rel)
-
-        w1_codes, w1_scales = quantise_weight(round_weight(w1_raw, "w1_grouped", "x_scale_tab", P), "w1")
-        x_codes = sb.tile([P, PICKED], U32, name="x_codes", tag="x_scale_tab", align_bytes=64)
-        y_banks = []
-        for h in range(2):
-            picks = slice(HALF * h, HALF * (h + 1))
-            nc.vector.tensor_copy(
-                x_codes[:, picks], x_word_tab[:].bitcast(U32).indirect(offs_t[:, HALF_COLS * h : HALF_COLS * (h + 1)])
-            )
-            pair = []
-            for b in range(2):
-                bank = ps.tile([P, 2, HALF], F32, name="y_bank%d%d" % (h, b), tag="bank%d" % (4 + 2 * h + b))
-                for s in range(2):
-                    cols = slice(P * (2 * b + s), P * (2 * b + s + 1))
-                    nc.tensor.matmul_mx(
-                        out=bank[:, s, :], lhsT=w1_codes[:, cols].bitcast(FP8X4), lhsT_scale=w1_scales[:, cols],
-                        rhs=x_codes[:, picks].bitcast(FP8X4), rhs_scale=x_bytes[:, picks],
-                        start=True, stop=True,
-                    )
-                pair.append(bank)
-            y_banks.append(pair)
-
-        signed_unit = sb.tile([P, PACK], F32, name="signed_unit", tag="w1_raw", align_bytes=64)
+        signed_unit = sb.tile([P, PACK], F32, name="signed_unit")
         nc.vector.scalar_tensor_tensor(signed_unit[:], two_if_pos[:], -1.0, unit_t[:], ALU.add, ALU.mult)
         for_max = sb.tile([P, PACK], F32, name="for_max")
         nc.vector.scalar_tensor_tensor(for_max[:], signed_unit[:], 0.5, signed_unit[:], ALU.mult, ALU.max)
         for_min = sb.tile([P, PACK], F32, name="for_min")
         nc.vector.scalar_tensor_tensor(for_min[:], signed_unit[:], 0.5, signed_unit[:], ALU.mult, ALU.min)
 
+        def round_weight(raw, name, copies):
+            grouped = sb.tile([P, PACK * PICKED], BF16, name=name + "_grouped", align_bytes=64)
+            dst = grouped[:].rearrange("p (t m j) -> p m j t", t=PACK, j=PACK)
+            src = raw[:].rearrange("p j (m t) -> p m j t", t=PACK)
+            for u in range(2):
+                copies[u](dst[:, :, :, 2 * u : 2 * u + 2], src[:, :, :, 2 * u : 2 * u + 2])
+            return grouped
+
+        def quantise_weight(grouped, name):
+            codes = sb.tile([P, PICKED], U32, name=name + "_codes", align_bytes=64)
+            scales = sb.tile([P, PICKED], U8, name=name + "_scales", align_bytes=64)
+            for u in range(2):
+                cols = slice(HALF * u, HALF * (u + 1))
+                nc.vector.quantize_mx(
+                    out=codes[:, cols].bitcast(FP8X4),
+                    scales=scales[:, cols],
+                    in_=grouped[:, PACK * HALF * u : PACK * HALF * (u + 1)],
+                )
+            return codes, scales
+
+        def half_list(t, u):
+            return t[:, HALF_COLS * u : HALF_COLS * (u + 1)]
+
+        e_bytes = sb.tile([P, PICKED], U8, name="e_bytes", align_bytes=64)
+        nc.vector.tensor_copy(e_bytes[:], e_scale_tab[:].indirect(tgt_t[:]))
+        w2_grouped = round_weight(w2_raw, "w2", (nc.vector.tensor_copy, nc.scalar.copy))
+        w2_codes, w2_scales = quantise_weight(w2_grouped, "w2")
+        fert_tab = sb.tile([P, TABLE], F32, name="fert_tab", tag="w2_raw", align_bytes=64)
+        nc.sync.dma_start(fert_tab[:], fert)
+
+        def first_product(codes, scales, picked_codes, picked_bytes, name, first_bank):
+            banks = []
+            for t in range(PACK):
+                bank = ps.tile([P, HALF], F32, name="%s_bank%d" % (name, t), tag="bank%d" % (first_bank + t))
+                cols = slice(P * t, P * (t + 1))
+                nc.tensor.matmul_mx(
+                    out=bank[:], lhsT=codes[:, cols].bitcast(FP8X4), lhsT_scale=scales[:, cols],
+                    rhs=picked_codes.bitcast(FP8X4), rhs_scale=picked_bytes, start=True, stop=True,
+                )
+                banks.append(bank)
+            return banks
+
+        ye = sb.tile([P, PACK, PICKED], F32, name="ye")
+        ye_banks = []
+        for g in range(2):
+            e_codes = sb.tile([P, HALF], U32, name="e_codes%d" % g, align_bytes=64)
+            nc.vector.tensor_copy(e_codes[:], e_word_tab[:].bitcast(U32).indirect(half_list(tgt_t, g)))
+            ye_banks.append(
+                first_product(w2_codes, w2_scales, e_codes[:], e_bytes[:, HALF * g : HALF * (g + 1)], "ye%d" % g, PACK * g)
+            )
+        x_bytes = []
+        for h, tag in enumerate(("e_word_tab", "x_bytes1")):
+            picked = sb.tile([P, HALF], U8, name="x_bytes%d" % h, tag=tag, align_bytes=64)
+            nc.vector.tensor_copy(picked[:], x_scale_tab[:].indirect(half_list(offs_t, h)))
+            x_bytes.append(picked)
+
+        def related_forms(rel, first, count):
+            for t in range(PACK):
+                picks = mor_t[:, first // 16 : (first + count) // 16]
+                nc.scalar.activation(rel[:, t, :], ye[:, t, :].indirect(picks), ACT.Copy, scale=0.7)
+
+        for g in range(2):
+            for t in range(PACK):
+                nc.scalar.activation(
+                    ye[:, t, HALF * g : HALF * (g + 1)], ye_banks[g][t][:], ACT.Copy, scale=abs_unit2[:, t : t + 1]
+                )
+        related0 = sb.tile([P, PACK, HALF], F32, name="related0")
+        related_forms(related0[:], 0, HALF)
+
+        w1_grouped = round_weight(w1_raw, "w1", (nc.vector.tensor_copy, nc.vector.tensor_copy))
+        w1_codes, w1_scales = quantise_weight(w1_grouped, "w1")
+        y_banks = []
+        for h in range(2):
+            x_codes = sb.tile([P, HALF], U32, name="x_codes%d" % h, align_bytes=64)
+            nc.vector.tensor_copy(x_codes[:], x_word_tab[:].bitcast(U32).indirect(half_list(offs_t, h)))
+            y_banks.append(
+                first_product(w1_codes, w1_scales, x_codes[:], x_bytes[h][:], "y%d" % h, PACK * h)
+            )
+
         hid2 = sb.tile([P, PACK * PICKED], BF16, name="hid2", tag="x_word_tab", align_bytes=64)
-        hid2_codes = sb.tile([P, PICKED], U32, name="hid2_codes", align_bytes=64)
+        hid2_codes = sb.tile([P, PICKED], U32, name="hid2_codes", tag="hid2_codes", align_bytes=64)
         hid2_scales = sb.tile([P, PICKED], U8, name="hid2_scales", align_bytes=64)
-        for u in range(2):
-            cols = slice(HALF * u, HALF * (u + 1))
-            part = hid2[:, PACK * HALF * u : PACK * HALF * (u + 1)]
+
+        def target_columns(rel, first, count):
+            cols = slice(first, first + count)
+            part = hid2[:, PACK * first : PACK * (first + count)]
             nc.vector.tensor_tensor(
-                part.rearrange("p (c i t) -> p c t i", i=4, t=PACK),
-                ye[:, :, cols].rearrange("p t (c i) -> p c t i", i=4),
-                related[u][:].rearrange("p t (c i) -> p c t i", i=4),
+                part.rearrange("p (c i t) -> p c t i", i=2, t=PACK),
+                ye[:, :, cols].rearrange("p t (c i) -> p c t i", i=2),
+                rel.rearrange("p t (c i) -> p c t i", i=2),
                 ALU.max,
             )
             nc.vector.quantize_mx(out=hid2_codes[:, cols].bitcast(FP8X4), scales=hid2_scales[:, cols], in_=part)
 
         def pairs_of(h, t):
-            return y_banks[h][t // 2][:].rearrange("p s (v d) -> p s d v", d=2)[:, t % 2]
+            return y_banks[h][t][:].rearrange("p (v d) -> p d v", d=2)
 
-        odd = []
-        for h in range(2):
+        def odd_tokens(h):
             odd_max = sb.tile([P, PACK, P], F32, name="odd_max%d" % h, tag="odd_max%d" % h)
             odd_min = sb.tile([P, PACK, P], F32, name="odd_min%d" % h)
             for t in range(PACK):
                 nc.scalar.activation(odd_max[:, t, :], pairs_of(h, t)[:, 1, :], ACT.Copy, scale=for_max[:, t : t + 1])
                 nc.scalar.activation(odd_min[:, t, :], pairs_of(h, t)[:, 1, :], ACT.Copy, scale=for_min[:, t : t + 1])
-            odd.append((odd_max, odd_min))
+            return odd_max, odd_min
 
-        def scores(h):
-            larger = sb.tile([P, PACK, P], F32, name="larger%d" % h)
+        def source_words(h, odd_max, odd_min):
+            larger = sb.tile([P, PACK, P], F32, name="larger%d" % h, tag="larger%d" % h, align_bytes=64)
             smaller = sb.tile([P, PACK, P], F32, name="smaller%d" % h)
             for t in range(PACK):
                 even = pairs_of(h, t)[:, 0, :]
-                nc.vector.scalar_tensor_tensor(larger[:, t, :], even, for_max[:, t : t + 1], odd[h][0][:, t, :], ALU.mult, ALU.max)
-                nc.vector.scalar_tensor_tensor(smaller[:, t, :], even, for_min[:, t : t + 1], odd[h][1][:, t, :], ALU.mult, ALU.min)
+                nc.vector.scalar_tensor_tensor(larger[:, t, :], even, for_max[:, t : t + 1], odd_max[:, t, :], ALU.mult, ALU.max)
+                nc.vector.scalar_tensor_tensor(smaller[:, t, :], even, for_min[:, t : t + 1], odd_min[:, t, :], ALU.mult, ALU.min)
             hid = sb.tile([P, PACK * P], BF16, name="hid%d" % h, align_bytes=64)
             nc.vector.tensor_tensor(
-                hid[:].rearrange("p (c i t) -> p c t i", i=4, t=PACK),
-                larger[:].rearrange("p t (c i) -> p c t i", i=4),
-                smaller[:].rearrange("p t (c i) -> p c t i", i=4),
+                hid[:].rearrange("p (c i t) -> p c t i", i=2, t=PACK),
+                larger[:].rearrange("p t (c i) -> p c t i", i=2),
+                smaller[:].rearrange("p t (c i) -> p c t i", i=2),
                 ALU.add,
             )
             hid_codes = sb.tile([P, P], U32, name="hid_codes%d" % h, align_bytes=64)
             hid_scales = sb.tile([P, P], U8, name="hid_scales%d" % h, align_bytes=64)
             nc.vector.quantize_mx(out=hid_codes[:].bitcast(FP8X4), scales=hid_scales[:], in_=hid[:])
+            return hid_codes, hid_scales
+
+        def exponentials(h, hid_codes, hid_scales):
             sc = ps.tile([P, PICKED], F32, name="sc%d" % h, tag="bank%d" % h)
             nc.tensor.matmul_mx(
                 out=sc[:], lhsT=hid_codes[:].bitcast(FP8X4), lhsT_scale=hid_scales[:],
                 rhs=hid2_codes[:].bitcast(FP8X4), rhs_scale=hid2_scales[:], start=True, stop=True,
             )
-            return sc
-
-        def exponentials(h, sc):
             neg_top = sb.tile([P, 1], F32, name="neg_top%d" % h)
             nc.vector.tensor_reduce(neg_top[:], sc[:], mybir.AxisListType.X, ALU.max, negate=True)
             ew = sb.tile([P, PICKED], F32, name="ew%d" % h)
@@ -209,26 +223,35 @@ def tile_picked_ywordal_fert_p_kernel(
             nc.scalar.activation(ew[:], sc[:], ACT.Exp, bias=neg_top[:], accum_out=tot[:])
             other = sb.tile([P, PICKED], F32, name="other%d" % h)
             for u in range(2):
-                nc.scalar.activation(
-                    other[:, HALF * u : HALF * (u + 1)],
-                    ew[:].indirect(dia_t[:, HALF_COLS * u : HALF_COLS * (u + 1)]), ACT.Copy, scale=-25.0,
-                )
+                nc.scalar.activation(other[:, HALF * u : HALF * (u + 1)], ew[:].indirect(half_list(dia_t, u)), ACT.Copy, scale=-25.0)
             return ew, tot, other
 
-        def finish(h, ew, tot, other):
+        def finish(h, ew, tot, other, own_tag, both_tag):
             inv_tot = sb.tile([P, 1], F32, name="inv_tot%d" % h)
             nc.vector.reciprocal(inv_tot[:], tot[:])
-            own = sb.tile([P, PICKED], F32, name="own%d" % h)
-            nc.vector.scalar_tensor_tensor(own[:], ew[:], inv_tot[:], fert50[:], ALU.mult, ALU.mult)
+            own = sb.tile([P, PICKED], F32, name="own%d" % h, tag=own_tag, align_bytes=64)
+            nc.vector.tensor_tensor(own[:], ew[:], fert50[:], ALU.mult)
+            both = sb.tile([P, PICKED], F32, name="both%d" % h, tag=both_tag, align_bytes=64)
             res = sb.tile([P, PICKED], F32, name="res%d" % h)
-            nc.vector.scalar_tensor_tensor(res[:], other[:], inv_tot[:], own[:], ALU.mult, ALU.add)
-            nc.sync.dma_start(out[P * h : P * (h + 1), :], res[:])
+            for u in range(2):
+                cols = slice(HALF * u, HALF * (u + 1))
+                nc.vector.tensor_tensor(both[:, cols], own[:, cols], other[:, cols], ALU.add)
+                nc.vector.tensor_scalar(res[:, cols], both[:, cols], inv_tot[:], None, ALU.mult)
+                nc.sync.dma_start(out[P * h : P * (h + 1), cols], res[:, cols])
 
-        sc0 = scores(0)
+        target_columns(related0[:], 0, HALF)
+        odd0 = odd_tokens(0)
+        related1 = sb.tile([P, 2, PACK, P], F32, name="related1", tag="e_word_tab", align_bytes=64)
+        for q in range(2):
+            related_forms(related1[:, q], HALF + P * q, P)
+        odd1 = odd_tokens(1)
+        hid0 = source_words(0, *odd0)
+        for q in range(2):
+            target_columns(related1[:, q], HALF + P * q, P)
         fert50 = sb.tile([P, PICKED], F32, name="fert50", tag="odd_max0")
         nc.scalar.activation(fert50[:], fert_tab[:].indirect(tgt_t[:]), ACT.Copy, scale=50.0)
-        soft0 = exponentials(0, sc0)
-        sc1 = scores(1)
-        soft1 = exponentials(1, sc1)
-        finish(0, *soft0)
-        finish(1, *soft1)
+        soft0 = exponentials(0, *hid0)
+        hid1 = source_words(1, *odd1)
+        soft1 = exponentials(1, *hid1)
+        finish(0, *soft0, "larger1", "hid2_codes")
+        finish(1, *soft1, "own1", "both1")

@@ -20,6 +20,8 @@ HALF = 256
 LIST_COLS = PICKED // 16
 HALF_COLS = HALF // 16
 
+OUT_PIECES = (((0, 256), (256, 512)), ((0, 256), (256, 384), (384, 512)))
+
 FLOPS = 2 * 512 * 512 * 512 * 2 + 2 * 256 * 512 * 512
 
 
@@ -222,21 +224,21 @@ def tile_picked_ywordal_fert_p_kernel(
             tot = sb.tile([P, 1], F32, name="tot%d" % h)
             nc.scalar.activation(ew[:], sc[:], ACT.Exp, bias=neg_top[:], accum_out=tot[:])
             other = sb.tile([P, PICKED], F32, name="other%d" % h)
-            for u in range(2):
-                nc.scalar.activation(other[:, HALF * u : HALF * (u + 1)], ew[:].indirect(half_list(dia_t, u)), ACT.Copy, scale=-25.0)
+            for first, end in OUT_PIECES[h]:
+                nc.scalar.activation(other[:, first:end], ew[:].indirect(dia_t[:, first // 16 : end // 16]), ACT.Copy, scale=-25.0)
             return ew, tot, other
 
-        def finish(h, ew, tot, other, own_tag, both_tag):
+        def finish(h, ew, tot, other, own_tag, res_tag):
             inv_tot = sb.tile([P, 1], F32, name="inv_tot%d" % h)
             nc.vector.reciprocal(inv_tot[:], tot[:])
             own = sb.tile([P, PICKED], F32, name="own%d" % h, tag=own_tag, align_bytes=64)
-            nc.vector.tensor_tensor(own[:], ew[:], fert50[:], ALU.mult)
-            both = sb.tile([P, PICKED], F32, name="both%d" % h, tag=both_tag, align_bytes=64)
-            res = sb.tile([P, PICKED], F32, name="res%d" % h)
             for u in range(2):
                 cols = slice(HALF * u, HALF * (u + 1))
-                nc.vector.tensor_tensor(both[:, cols], own[:, cols], other[:, cols], ALU.add)
-                nc.vector.tensor_scalar(res[:, cols], both[:, cols], inv_tot[:], None, ALU.mult)
+                nc.vector.scalar_tensor_tensor(own[:, cols], ew[:, cols], inv_tot[:], fert50[:, cols], ALU.mult, ALU.mult)
+            res = sb.tile([P, PICKED], F32, name="res%d" % h, tag=res_tag, align_bytes=64)
+            for first, end in OUT_PIECES[h]:
+                cols = slice(first, end)
+                nc.vector.scalar_tensor_tensor(res[:, cols], other[:, cols], inv_tot[:], own[:, cols], ALU.mult, ALU.add)
                 nc.sync.dma_start(out[P * h : P * (h + 1), cols], res[:, cols])
 
         target_columns(related0[:], 0, HALF)
@@ -254,4 +256,4 @@ def tile_picked_ywordal_fert_p_kernel(
         hid1 = source_words(1, *odd1)
         soft1 = exponentials(1, *hid1)
         finish(0, *soft0, "larger1", "hid2_codes")
-        finish(1, *soft1, "own1", "both1")
+        finish(1, *soft1, "own1", "res1")

from contextlib import ExitStack

import concourse.mybir as mybir

F32 = mybir.dt.float32
BF16 = mybir.dt.bfloat16
I32 = mybir.dt.int32
U32 = mybir.dt.uint32
U16 = mybir.dt.uint16
U8 = mybir.dt.uint8
FP8X4 = mybir.dt.float8_e4m3fn_x4
ALU = mybir.AluOpType
ACT = mybir.ActivationFunctionType

P = 128
PACK = 4
TABLE = 2048
PICKED = 512
HALF = 256
LIST_COLS = PICKED // 16
HALF_COLS = HALF // 16

OUT_PIECES = (((0, 256), (256, 512)), ((0, 256), (256, 384), (384, 512)))

FLOPS = 2 * 512 * 512 * 512 * 2 + 2 * 256 * 512 * 512


def tile_picked_ywordal_fert_p_kernel(
    tc, x_words, x_scales, w1, e_words, e_scales, w2, unit, unit2, fert, offs, tgt, mor, dia, out
):
    nc = tc.nc
    with ExitStack() as ctx:
        sb = ctx.enter_context(tc.tile_pool(name="sb", bufs=1))
        ps = ctx.enter_context(tc.psum_pool(name="ps", bufs=1))

        def load_list(src, name):
            t = sb.tile([P, LIST_COLS], U16, name=name)
            nc.sync.dma_start(t[:], src)
            return t

        def load_words(src, name, tag):
            t = sb.tile([P, TABLE], I32, name=name, tag=tag, align_bytes=64)
            nc.sync.dma_start(t[:], src[0].rearrange("p n r -> p (n r)").bitcast(I32))
            return t

        def cleared_scale_table(name):
            t = sb.tile([P, TABLE], U8, name=name, tag=name, align_bytes=64)
            nc.vector.memset(t[:].bitcast(I32), 0)
            return t

        def load_scales(t, src):
            for r in range(4):
                nc.sync.dma_start(t[r:P:32, :].bitcast(I32), src[0, r:16:4, :].bitcast(I32))

        def load_weight(src, name, tag):
            t = sb.tile([P, PACK, PICKED], F32, name=name, tag=tag, align_bytes=64)
            nc.sync.dma_start(t[:], src.rearrange("(p j) c -> p j c", j=PACK))
            return t

        def load_factor(src, name):
            t = sb.tile([P, PACK], F32, name=name, tag=name, align_bytes=64)
            nc.sync.dma_start(t[:], src.rearrange("(p t) o -> p (t o)", t=PACK))
            return t

        e_scale_tab = cleared_scale_table("e_scale_tab")
        x_scale_tab = cleared_scale_table("x_scale_tab")
        tgt_t = load_list(tgt, "tgt_t")
        unit2_t = load_factor(unit2, "unit2_t")
        unit_t = load_factor(unit, "unit_t")
        w2_raw = load_weight(w2, "w2_raw", "w2_raw")
        load_scales(e_scale_tab, e_scales)
        offs_t = load_list(offs, "offs_t")
        mor_t = load_list(mor, "mor_t")
        e_word_tab = load_words(e_words, "e_word_tab", "e_word_tab")
        load_scales(x_scale_tab, x_scales)
        w1_raw = load_weight(w1, "w1_raw", "w1_raw")
        dia_t = load_list(dia, "dia_t")
        x_word_tab = load_words(x_words, "x_word_tab", "x_word_tab")

        two_if_pos = sb.tile([P, PACK], F32, name="two_if_pos")
        nc.vector.tensor_scalar(two_if_pos[:], unit2_t[:], 0.0, 2.0, ALU.is_ge, ALU.mult)
        abs_unit2 = sb.tile([P, PACK], F32, name="abs_unit2")
        nc.vector.scalar_tensor_tensor(abs_unit2[:], two_if_pos[:], -1.0, unit2_t[:], ALU.add, ALU.mult)
        signed_unit = sb.tile([P, PACK], F32, name="signed_unit")
        nc.vector.scalar_tensor_tensor(signed_unit[:], two_if_pos[:], -1.0, unit_t[:], ALU.add, ALU.mult)
        for_max = sb.tile([P, PACK], F32, name="for_max")
        nc.vector.scalar_tensor_tensor(for_max[:], signed_unit[:], 0.5, signed_unit[:], ALU.mult, ALU.max)
        for_min = sb.tile([P, PACK], F32, name="for_min")
        nc.vector.scalar_tensor_tensor(for_min[:], signed_unit[:], 0.5, signed_unit[:], ALU.mult, ALU.min)

        def round_weight(raw, name, copies):
            grouped = sb.tile([P, PACK * PICKED], BF16, name=name + "_grouped", align_bytes=64)
            dst = grouped[:].rearrange("p (t m j) -> p m j t", t=PACK, j=PACK)
            src = raw[:].rearrange("p j (m t) -> p m j t", t=PACK)
            for u in range(2):
                copies[u](dst[:, :, :, 2 * u : 2 * u + 2], src[:, :, :, 2 * u : 2 * u + 2])
            return grouped

        def quantise_weight(grouped, name):
            codes = sb.tile([P, PICKED], U32, name=name + "_codes", align_bytes=64)
            scales = sb.tile([P, PICKED], U8, name=name + "_scales", align_bytes=64)
            for u in range(2):
                cols = slice(HALF * u, HALF * (u + 1))
                nc.vector.quantize_mx(
                    out=codes[:, cols].bitcast(FP8X4),
                    scales=scales[:, cols],
                    in_=grouped[:, PACK * HALF * u : PACK * HALF * (u + 1)],
                )
            return codes, scales

        def half_list(t, u):
            return t[:, HALF_COLS * u : HALF_COLS * (u + 1)]

        e_bytes = sb.tile([P, PICKED], U8, name="e_bytes", align_bytes=64)
        nc.vector.tensor_copy(e_bytes[:], e_scale_tab[:].indirect(tgt_t[:]))
        w2_grouped = round_weight(w2_raw, "w2", (nc.vector.tensor_copy, nc.scalar.copy))
        w2_codes, w2_scales = quantise_weight(w2_grouped, "w2")
        fert_tab = sb.tile([P, TABLE], F32, name="fert_tab", tag="w2_raw", align_bytes=64)
        nc.sync.dma_start(fert_tab[:], fert)

        def first_product(codes, scales, picked_codes, picked_bytes, name, first_bank):
            banks = []
            for t in range(PACK):
                bank = ps.tile([P, HALF], F32, name="%s_bank%d" % (name, t), tag="bank%d" % (first_bank + t))
                cols = slice(P * t, P * (t + 1))
                nc.tensor.matmul_mx(
                    out=bank[:], lhsT=codes[:, cols].bitcast(FP8X4), lhsT_scale=scales[:, cols],
                    rhs=picked_codes.bitcast(FP8X4), rhs_scale=picked_bytes, start=True, stop=True,
                )
                banks.append(bank)
            return banks

        ye = sb.tile([P, PACK, PICKED], F32, name="ye")
        ye_banks = []
        for g in range(2):
            e_codes = sb.tile([P, HALF], U32, name="e_codes%d" % g, align_bytes=64)
            nc.vector.tensor_copy(e_codes[:], e_word_tab[:].bitcast(U32).indirect(half_list(tgt_t, g)))
            ye_banks.append(
                first_product(w2_codes, w2_scales, e_codes[:], e_bytes[:, HALF * g : HALF * (g + 1)], "ye%d" % g, PACK * g)
            )
        x_bytes = []
        for h, tag in enumerate(("e_word_tab", "x_bytes1")):
            picked = sb.tile([P, HALF], U8, name="x_bytes%d" % h, tag=tag, align_bytes=64)
            nc.vector.tensor_copy(picked[:], x_scale_tab[:].indirect(half_list(offs_t, h)))
            x_bytes.append(picked)

        def related_forms(rel, first, count):
            for t in range(PACK):
                picks = mor_t[:, first // 16 : (first + count) // 16]
                nc.scalar.activation(rel[:, t, :], ye[:, t, :].indirect(picks), ACT.Copy, scale=0.7)

        for g in range(2):
            for t in range(PACK):
                nc.scalar.activation(
                    ye[:, t, HALF * g : HALF * (g + 1)], ye_banks[g][t][:], ACT.Copy, scale=abs_unit2[:, t : t + 1]
                )
        related0 = sb.tile([P, PACK, HALF], F32, name="related0")
        related_forms(related0[:], 0, HALF)

        w1_grouped = round_weight(w1_raw, "w1", (nc.vector.tensor_copy, nc.vector.tensor_copy))
        w1_codes, w1_scales = quantise_weight(w1_grouped, "w1")
        y_banks = []
        for h in range(2):
            x_codes = sb.tile([P, HALF], U32, name="x_codes%d" % h, align_bytes=64)
            nc.vector.tensor_copy(x_codes[:], x_word_tab[:].bitcast(U32).indirect(half_list(offs_t, h)))
            y_banks.append(
                first_product(w1_codes, w1_scales, x_codes[:], x_bytes[h][:], "y%d" % h, PACK * h)
            )

        hid2 = sb.tile([P, PACK * PICKED], BF16, name="hid2", tag="x_word_tab", align_bytes=64)
        hid2_codes = sb.tile([P, PICKED], U32, name="hid2_codes", tag="hid2_codes", align_bytes=64)
        hid2_scales = sb.tile([P, PICKED], U8, name="hid2_scales", align_bytes=64)

        def target_columns(rel, first, count):
            cols = slice(first, first + count)
            part = hid2[:, PACK * first : PACK * (first + count)]
            nc.vector.tensor_tensor(
                part.rearrange("p (c i t) -> p c t i", i=2, t=PACK),
                ye[:, :, cols].rearrange("p t (c i) -> p c t i", i=2),
                rel.rearrange("p t (c i) -> p c t i", i=2),
                ALU.max,
            )
            nc.vector.quantize_mx(out=hid2_codes[:, cols].bitcast(FP8X4), scales=hid2_scales[:, cols], in_=part)

        def pairs_of(h, t):
            return y_banks[h][t][:].rearrange("p (v d) -> p d v", d=2)

        def odd_tokens(h):
            odd_max = sb.tile([P, PACK, P], F32, name="odd_max%d" % h, tag="odd_max%d" % h)
            odd_min = sb.tile([P, PACK, P], F32, name="odd_min%d" % h)
            for t in range(PACK):
                nc.scalar.activation(odd_max[:, t, :], pairs_of(h, t)[:, 1, :], ACT.Copy, scale=for_max[:, t : t + 1])
                nc.scalar.activation(odd_min[:, t, :], pairs_of(h, t)[:, 1, :], ACT.Copy, scale=for_min[:, t : t + 1])
            return odd_max, odd_min

        def source_words(h, odd_max, odd_min):
            larger = sb.tile([P, PACK, P], F32, name="larger%d" % h, tag="larger%d" % h, align_bytes=64)
            smaller = sb.tile([P, PACK, P], F32, name="smaller%d" % h)
            for t in range(PACK):
                even = pairs_of(h, t)[:, 0, :]
                nc.vector.scalar_tensor_tensor(larger[:, t, :], even, for_max[:, t : t + 1], odd_max[:, t, :], ALU.mult, ALU.max)
                nc.vector.scalar_tensor_tensor(smaller[:, t, :], even, for_min[:, t : t + 1], odd_min[:, t, :], ALU.mult, ALU.min)
            hid = sb.tile([P, PACK * P], BF16, name="hid%d" % h, align_bytes=64)
            nc.vector.tensor_tensor(
                hid[:].rearrange("p (c i t) -> p c t i", i=2, t=PACK),
                larger[:].rearrange("p t (c i) -> p c t i", i=2),
                smaller[:].rearrange("p t (c i) -> p c t i", i=2),
                ALU.add,
            )
            hid_codes = sb.tile([P, P], U32, name="hid_codes%d" % h, align_bytes=64)
            hid_scales = sb.tile([P, P], U8, name="hid_scales%d" % h, align_bytes=64)
            nc.vector.quantize_mx(out=hid_codes[:].bitcast(FP8X4), scales=hid_scales[:], in_=hid[:])
            return hid_codes, hid_scales

        def exponentials(h, hid_codes, hid_scales):
            sc = ps.tile([P, PICKED], F32, name="sc%d" % h, tag="bank%d" % h)
            nc.tensor.matmul_mx(
                out=sc[:], lhsT=hid_codes[:].bitcast(FP8X4), lhsT_scale=hid_scales[:],
                rhs=hid2_codes[:].bitcast(FP8X4), rhs_scale=hid2_scales[:], start=True, stop=True,
            )
            neg_top = sb.tile([P, 1], F32, name="neg_top%d" % h)
            nc.vector.tensor_reduce(neg_top[:], sc[:], mybir.AxisListType.X, ALU.max, negate=True)
            ew = sb.tile([P, PICKED], F32, name="ew%d" % h)
            tot = sb.tile([P, 1], F32, name="tot%d" % h)
            nc.scalar.activation(ew[:], sc[:], ACT.Exp, bias=neg_top[:], accum_out=tot[:])
            other = sb.tile([P, PICKED], F32, name="other%d" % h)
            for first, end in OUT_PIECES[h]:
                nc.scalar.activation(other[:, first:end], ew[:].indirect(dia_t[:, first // 16 : end // 16]), ACT.Copy, scale=-25.0)
            return ew, tot, other

        def finish(h, ew, tot, other, own_tag, res_tag):
            inv_tot = sb.tile([P, 1], F32, name="inv_tot%d" % h)
            nc.vector.reciprocal(inv_tot[:], tot[:])
            own = sb.tile([P, PICKED], F32, name="own%d" % h, tag=own_tag, align_bytes=64)
            for u in range(2):
                cols = slice(HALF * u, HALF * (u + 1))
                nc.vector.scalar_tensor_tensor(own[:, cols], ew[:, cols], inv_tot[:], fert50[:, cols], ALU.mult, ALU.mult)
            res = sb.tile([P, PICKED], F32, name="res%d" % h, tag=res_tag, align_bytes=64)
            for first, end in OUT_PIECES[h]:
                cols = slice(first, end)
                nc.vector.scalar_tensor_tensor(res[:, cols], other[:, cols], inv_tot[:], own[:, cols], ALU.mult, ALU.add)
                nc.sync.dma_start(out[P * h : P * (h + 1), cols], res[:, cols])

        target_columns(related0[:], 0, HALF)
        odd0 = odd_tokens(0)
        related1 = sb.tile([P, 2, PACK, P], F32, name="related1", tag="e_word_tab", align_bytes=64)
        for q in range(2):
            related_forms(related1[:, q], HALF + P * q, P)
        odd1 = odd_tokens(1)
        hid0 = source_words(0, *odd0)
        for q in range(2):
            target_columns(related1[:, q], HALF + P * q, P)
        fert50 = sb.tile([P, PICKED], F32, name="fert50", tag="odd_max0")
        nc.scalar.activation(fert50[:], fert_tab[:].indirect(tgt_t[:]), ACT.Copy, scale=50.0)
        soft0 = exponentials(0, *hid0)
        hid1 = source_words(1, *odd1)
        soft1 = exponentials(1, *hid1)
        finish(0, *soft0, "larger1", "hid2_codes")
        finish(1, *soft1, "own1", "res1")
